import numpy as np
import ml_dtypes


def mxq(x, axis, fmt="e4m3"):
    dtype, down = {"e4m3": (ml_dtypes.float8_e4m3fn, 7), "e5m2": (ml_dtypes.float8_e5m2, 14)}[fmt]
    v = np.moveaxis(np.asarray(x, np.float32).astype(ml_dtypes.bfloat16).astype(np.float64), axis, -1)
    blocks = v.reshape(v.shape[:-1] + (-1, 32))
    amax = np.abs(blocks).max(-1, keepdims=True)
    byte = np.maximum(np.where(amax > 0, np.frexp(amax)[1] - 1 + 127, 0) - down, 1)
    scale = np.exp2(byte - 127.0)
    codes = (blocks / scale).astype(np.float32).astype(dtype).astype(np.float64)
    return np.moveaxis((codes * scale).reshape(v.shape), -1, axis)


WIDE = False


def mx_kscale(k):
    if not WIDE:
        return np.ones(k)
    levels = np.array([10, -10, 5, -5, 0])
    if k % 512:
        return np.exp2(np.random.permutation(np.resize(levels, k // 32))).repeat(32)
    a = np.empty((k // 512, 16))
    for p in range(k // 512):
        a[p, :8] = np.random.permutation(np.resize(levels, 8))
        for g in range(8):
            far = levels[np.abs(levels - a[p, g]) >= 10]
            a[p, g + 8] = far[np.random.randint(len(far))]
    return np.exp2(a.ravel()).repeat(32)


def f64(x):
    return np.asarray(x).astype(np.float64)


def striped(idx):
    return np.tile(idx.reshape(-1, 16).T, (8, 1)).astype(np.uint16)


def unstriped(offs):
    return offs[:16].T.reshape(-1).astype(np.int64)


def striped8(idx):
    return np.concatenate([x.reshape(-1, 16).T for x in idx]).astype(np.uint16)


def runs(offs, k):
    lists = np.stack([offs[16 * r : 16 * r + 16].T.reshape(-1) for r in range(8)]).astype(np.int64)
    return lists[np.arange(k) % 512 // 64]


def pack_weight(w):
    k, n = w.shape
    w = f64(np.asarray(w, np.float32).astype(ml_dtypes.bfloat16)).reshape(k // 32, 32, n)
    amax = np.abs(w).max(1)
    byte = np.clip(np.where(amax > 0, np.frexp(amax)[1] - 1 + 127 - 7, 1), 1, 254)
    scaled = (w * np.exp2(127.0 - byte)[:, None, :]).reshape(k, n).astype(np.float32)
    words = np.ascontiguousarray(scaled.reshape(k // 512, 128, 4, n).transpose(0, 1, 3, 2)).astype(ml_dtypes.float8_e4m3fn).view(np.uint8)
    return words, np.ascontiguousarray(byte.astype(np.uint8).reshape(k // 512, 16, n))


def unpack_weight(words, scales):
    g, p, n, _ = words.shape
    vals = np.ascontiguousarray(words).view(ml_dtypes.float8_e4m3fn).astype(np.float64) * np.repeat(np.exp2(scales.astype(np.float64) - 127.0), 8, axis=1)[..., None]
    return vals.transpose(0, 1, 3, 2).reshape(g * 512, n)


def sigmoid(v):
    return 1.0 / (1.0 + np.exp(-np.maximum(v, -700.0)))


K, T, S, N, H, G = 512, 1024, 512, 512, 512, 2048


def setup_inputs():
    n = np.random.standard_normal
    s = mx_kscale(K)[:, None]
    u = mx_kscale(S)
    packed_xT = pack_weight(n((K, T)) * s)
    packed_dT = pack_weight(n((K, G)) / s)
    return {
        "x_words": packed_xT[0],
        "x_scales": packed_xT[1],
        "w1": (n((K, H)) / np.sqrt(K) / s).astype(np.float32),
        "d_words": packed_dT[0],
        "d_scales": packed_dT[1],
        "gn": (np.random.uniform(0.5, 1.5, (H, 1)) * u[:, None]).astype(np.float32),
        "gk": (np.random.uniform(0.5, 1.5, (H, 1)) * u[:, None]).astype(np.float32),
        "w2": (n((H, N)) / np.sqrt(2 * H) / u[:, None]).astype(np.float32),
        "w3": (n((H, N)) / np.sqrt(2 * H) / u[:, None]).astype(np.float32),
        "offs": striped(np.random.permutation(T)[:S]),
        "kidx": striped8(np.random.randint(0, G, (8, H))),
        "two": striped(np.random.permutation(T)[:S]),
        "n1": striped8(np.stack([np.random.permutation(S) for _ in range(8)])),
        "n2": striped(np.random.permutation(S)),
        "n3": striped(np.random.permutation(S)),
        "n4": striped(np.random.permutation(S)),
        "n5": striped(np.random.permutation(S)),
        "n6": striped(np.random.permutation(S)),
    }


def reference(x_words, x_scales, w1, d_words, d_scales, gn, gk, w2, w3, offs, kidx, two, n1, n2, n3, n4, n5, n6):
    xq = unpack_weight(x_words, x_scales)[:, unstriped(offs)]
    y = mxq(f64(w1), 0, "e4m3").T @ xq
    st = y * (sigmoid(y[np.arange(H)[:, None], runs(n1, H)]))
    z = f64(gn) * (np.maximum(st, st[np.arange(H)[:, None], runs(n1, H)]))
    d_kidx = unpack_weight(d_words, d_scales)[np.arange(K)[:, None], runs(kidx, K)]
    x_two = unpack_weight(x_words, x_scales)[:, unstriped(two)]
    s = 0.0625 * (d_kidx.T @ x_two)
    ex = np.exp(0.5 * s)
    z2 = f64(gk) * (np.log((ex + ex[:, unstriped(n2)]) / (ex[:, unstriped(n3)] + ex[:, unstriped(n4)])))
    h = mxq(f64(w2), 0, "e4m3").T @ mxq(z, 0, "e4m3") + mxq(f64(w3), 0, "e4m3").T @ mxq(z2, 0, "e4m3")
    return (h - h[:, unstriped(n5)]) / (np.abs(h[:, unstriped(n6)] - h) + 0.5)

@@ -1,0 +1,206 @@
+from contextlib import ExitStack
+
+import concourse.mybir as mybir
+
+K, T, S, N, H, G = 512, 1024, 512, 512, 512, 2048
+FLOPS = 4 * 2 * 512 * 512 * 512
+
+F32 = mybir.dt.float32
+BF16 = mybir.dt.bfloat16
+I32 = mybir.dt.int32
+U32 = mybir.dt.uint32
+U16 = mybir.dt.uint16
+U8 = mybir.dt.uint8
+FP8X4 = mybir.dt.float8_e4m3fn_x4
+ALU = mybir.AluOpType
+ACT = mybir.ActivationFunctionType
+
+P = 128
+PACK = 4
+WIDE = 2 * S
+NARROW = S + 32
+
+
+def tile_picked_jkeytwicpoddsfrac_none_p_kernel(
+    tc, x_words, x_scales, w1, d_words, d_scales, gn, gk, w2, w3, offs, kidx, two, n1, n2, n3, n4, n5, n6, out
+):
+    nc = tc.nc
+    with ExitStack() as ctx:
+        lists = ctx.enter_context(tc.tile_pool(name="lists", bufs=1))
+        keep = ctx.enter_context(tc.tile_pool(name="keep", bufs=1))
+        psum = ctx.enter_context(tc.psum_pool(name="psum", bufs=1))
+
+        def load_list(name, src):
+            tile = lists.tile([P, S // 16], U16, name=name)
+            nc.sync.dma_start(tile[:], src)
+            return tile
+
+        def load_weight(name, tag, w):
+            raw = keep.tile([P, PACK, 512], F32, name=name, tag=tag, align_bytes=64)
+            nc.sync.dma_start(out=raw[:], in_=w.rearrange("(p j) n -> p j n", j=PACK))
+            return raw
+
+        def quantize(name, grouped):
+            codes = keep.tile([P, 512], U32, name=name + "_codes", align_bytes=64)
+            scales = keep.tile([P, 512], U8, name=name + "_scales", align_bytes=64)
+            nc.vector.quantize_mx(out=codes[:].bitcast(FP8X4), scales=scales[:], in_=grouped[:])
+            return codes, scales
+
+        def gather(name, dtype, window, offsets):
+            picked = keep.tile([P, S], dtype, name=name, tag=name, align_bytes=64)
+            nc.vector.tensor_copy(picked[:], window.indirect(offsets[:]))
+            return picked
+
+        def product(bank, lhs, cols, rhs, start, stop):
+            nc.tensor.matmul_mx(
+                out=bank[:],
+                lhsT=lhs[0][:, cols].bitcast(FP8X4),
+                lhsT_scale=lhs[1][:, cols],
+                rhs=rhs[0][:].bitcast(FP8X4),
+                rhs_scale=rhs[1][:],
+                start=start,
+                stop=stop,
+            )
+
+        def interleave(engine_copy, grouped, planes):
+            engine_copy(
+                out=grouped[:].rearrange("p (c i t) -> p c t i", i=4, t=PACK),
+                in_=planes[:].rearrange("p t (c i) -> p c t i", i=4),
+            )
+
+        xs = keep.tile([P, T], U8, name="xs")
+        ds = keep.tile([P, G], U8, name="ds")
+        dd_s = keep.tile([P, S], U8, name="dd_s", tag="dd_s", align_bytes=64)
+        nc.gpsimd.memset(xs[:].bitcast(I32), 0)
+        nc.gpsimd.memset(ds[:].bitcast(I32), 0)
+        nc.gpsimd.memset(dd_s[:].bitcast(I32), 0)
+        gn_t = keep.tile([P, PACK], F32, name="gn_t")
+        gk_t = keep.tile([P, PACK], F32, name="gk_t")
+        nc.gpsimd.dma_start(out=gk_t[:], in_=gk.rearrange("(p t) o -> p (t o)", t=PACK))
+        nc.gpsimd.dma_start(out=gn_t[:], in_=gn.rearrange("(p t) o -> p (t o)", t=PACK))
+
+        offs_t = load_list("offs_t", offs)
+        for r in range(4):
+            nc.sync.dma_start(out=xs[r:P:32, :].bitcast(I32), in_=x_scales[0, r:16:4, :].bitcast(I32))
+        xw = keep.tile([P, T], I32, name="xw")
+        nc.sync.dma_start(out=xw[:], in_=x_words[0].rearrange("p n t -> p (n t)").bitcast(I32))
+        w1_raw = load_weight("w1_raw", "xt_w", w1)
+        kidx_t = load_list("kidx_t", kidx)
+        for e in range(2):
+            nc.sync.dma_start(out=ds[e:P:16, :].bitcast(I32), in_=d_scales[0, e:16:2, :].bitcast(I32))
+        two_t = load_list("two_t", two)
+        dw = keep.tile([P, G], I32, name="dw", tag="dw", align_bytes=64)
+        nc.sync.dma_start(out=dw[:], in_=d_words[0].rearrange("p n t -> p (n t)").bitcast(I32))
+        n1_t = load_list("n1_t", n1)
+        n3_t = load_list("n3_t", n3)
+        n2_t = load_list("n2_t", n2)
+        n4_t = load_list("n4_t", n4)
+        n6_t = load_list("n6_t", n6)
+        n5_t = load_list("n5_t", n5)
+
+        xo_s = gather("xo_s", U8, xs[:], offs_t)
+        xo_w = gather("xo_w", U32, xw[:].bitcast(U32), offs_t)
+        w1_b = keep.tile([P, 2048], BF16, name="w1_b", tag="dk_w", align_bytes=64)
+        nc.scalar.copy(
+            out=w1_b[:].rearrange("p (t m j) -> p m j t", t=PACK, j=PACK),
+            in_=w1_raw[:].rearrange("p j (m t) -> p m j t", t=PACK),
+        )
+        w1_q = quantize("w1", w1_b)
+        dk_s = gather("dk_s", U8, ds[:], kidx_t)
+        dealt_s = keep.tile([P, S], U8, name="dealt_s")
+        nc.vector.tensor_copy(
+            out=dealt_s[:].rearrange("p (t m) -> p t m", t=PACK), in_=dk_s[:].rearrange("p (m t) -> p t m", t=PACK)
+        )
+        for r in range(4):
+            src = 16 * (r // 2) + r % 2
+            nc.sync.dma_start(out=dd_s[r:P:32, :].bitcast(I32), in_=dealt_s[src:P:32, :].bitcast(I32))
+        w3_raw = load_weight("w3_raw", "dk_s", w3)
+        xt_s = gather("xt_s", U8, xs[:], two_t)
+        xt_w = gather("xt_w", U32, xw[:].bitcast(U32), two_t)
+        dk_w = gather("dk_w", U32, dw[:].bitcast(U32), kidx_t)
+        dd_w = keep.tile([P, S], U32, name="dd_w", tag="dd_w", align_bytes=64)
+        nc.vector.tensor_copy(
+            out=dd_w[:].rearrange("p (t m) -> p t m", t=PACK), in_=dk_w[:].rearrange("p (m t) -> p t m", t=PACK)
+        )
+        w2_raw = load_weight("w2_raw", "dw", w2)
+
+        y_ps = [psum.tile([P, S], F32, name="y_ps%d" % t, tag="bank%d" % t) for t in range(PACK)]
+        for t in range(PACK):
+            product(y_ps[t], w1_q, slice(P * t, P * (t + 1)), (xo_w, xo_s), True, True)
+
+        def tiles(name, width, dtype=F32):
+            return [keep.tile([P, width], dtype, name="%s%d" % (name, t), tag="%s%d" % (name, t), align_bytes=64) for t in range(PACK)]
+
+        sg, y, st = tiles("sg", WIDE), tiles("y", S), tiles("st", WIDE)
+        ex, ex2, num, g3, den = tiles("ex", NARROW), tiles("exb", S), tiles("num", S), tiles("gth", S), tiles("den", S)
+        z_planes = keep.tile([P, PACK, S], BF16, name="z_planes")
+        z2_planes = keep.tile([P, PACK, S], BF16, name="z2_planes")
+
+        for t in range(PACK):
+            nc.scalar.activation(sg[t][:, :S], y_ps[t][:], ACT.Sigmoid)
+            nc.scalar.copy(y[t][:], y_ps[t][:])
+            nc.vector.tensor_tensor(st[t][:, :S], sg[t][:].indirect(n1_t[:]), y[t][:], ALU.mult)
+        for t in range(PACK):
+            s_ps = psum.tile([P, S], F32, name="s_ps%d" % t, tag="bank%d" % t)
+            product(s_ps, (dd_w, dd_s), slice(P * t, P * (t + 1)), (xt_w, xt_s), True, True)
+            nc.scalar.activation(ex[t][:, :S], s_ps[:], ACT.Exp, scale=0.03125)
+            nc.sync.dma_start(out=ex2[t][:], in_=ex[t][:, :S])
+        w3_b = keep.tile([P, 2048], BF16, name="w3_b", tag="dk_w", align_bytes=64)
+        interleave(nc.vector.tensor_copy, w3_b, w3_raw)
+        for t in range(PACK):
+            nc.scalar.activation(g3[t][:], ex[t][:].indirect(n3_t[:]), ACT.Copy)
+        w3_q = quantize("w3", w3_b)
+        for t in range(PACK):
+            nc.vector.tensor_tensor(num[t][:], ex[t][:].indirect(n2_t[:]), ex2[t][:], ALU.add)
+        stg = [
+            keep.tile([P, S], F32, name="stg%d" % t, tag=tag, align_bytes=64)
+            for t, tag in enumerate(("xt_w", "dd_w", "xt_s", "dd_s"))
+        ]
+        for t in range(PACK):
+            nc.scalar.activation(stg[t][:], st[t][:].indirect(n1_t[:]), ACT.Copy)
+        for t in range(PACK):
+            nc.vector.tensor_tensor(den[t][:], ex[t][:].indirect(n4_t[:]), g3[t][:], ALU.add)
+        for t in range(PACK):
+            nc.scalar.activation(num[t][:], num[t][:], ACT.Ln)
+        for t in range(PACK):
+            nc.vector.tensor_tensor(stg[t][:], stg[t][:], st[t][:, :S], ALU.max)
+        for t in range(PACK):
+            nc.scalar.activation(g3[t][:], den[t][:], ACT.Ln)
+            nc.vector.tensor_tensor(num[t][:], num[t][:], g3[t][:], ALU.subtract)
+            nc.vector.tensor_scalar(z2_planes[:, t, :], num[t][:], gk_t[:, t : t + 1], None, ALU.mult)
+        for t in range(PACK):
+            nc.scalar.activation(z_planes[:, t, :], stg[t][:], ACT.Copy, scale=gn_t[:, t : t + 1])
+        z2_b = keep.tile([P, 2048], BF16, name="z2_b", align_bytes=64)
+        interleave(nc.vector.tensor_copy, z2_b, z2_planes)
+        w2_b = keep.tile([P, 2048], BF16, name="w2_b", tag="ex3", align_bytes=64)
+        interleave(nc.scalar.copy, w2_b, w2_raw)
+        z_b = keep.tile([P, 2048], BF16, name="z_b", align_bytes=64)
+        interleave(nc.vector.tensor_copy, z_b, z_planes)
+        z2_q = quantize("z2", z2_b)
+        z_q = quantize("z", z_b)
+        w2_q = quantize("w2", w2_b)
+
+        h_ps = [psum.tile([P, S], F32, name="h_ps%d" % m) for m in range(PACK)]
+        for m in range(PACK):
+            product(h_ps[m], w3_q, slice(P * m, P * (m + 1)), z2_q, True, False)
+        for m in range(PACK):
+            product(h_ps[m], w2_q, slice(P * m, P * (m + 1)), z_q, False, True)
+
+        h, h2, d6 = tiles("h", WIDE), tiles("hb", S), tiles("dsix", S)
+        d5 = [h[(m - 1) % PACK][:, S:] for m in range(PACK)]
+        for m in range(PACK):
+            nc.scalar.copy(h[m][:, :S], h_ps[m][:])
+            if m in (0, PACK - 1):
+                nc.vector.tensor_copy(h2[m][:], h[m][:, :S])
+            else:
+                nc.scalar.copy(h2[m][:], h_ps[m][:])
+            nc.vector.tensor_tensor(d6[m][:], h[m][:].indirect(n6_t[:]), h2[m][:], ALU.subtract)
+        for m in range(PACK):
+            nc.scalar.activation(d6[m][:], d6[m][:], ACT.Abs)
+            nc.scalar.activation(d6[m][:], d6[m][:], ACT.Ln, bias=0.5)
+        for m in range(PACK):
+            nc.vector.tensor_tensor(d5[m], h[m][:].indirect(n5_t[:]), h2[m][:], ALU.subtract)
+        for m in range(PACK):
+            nc.scalar.activation(d6[m][:], d6[m][:], ACT.Exp, scale=-1.0)
+            nc.vector.scalar_tensor_tensor(h2[m][:], d5[m], -1.0, d6[m][:], ALU.mult, ALU.mult)
+            nc.sync.dma_start(out=out[P * m : P * (m + 1), :], in_=h2[m][:])

@@ -19,6 +19,7 @@ P = 128
 PACK = 4
 WIDE = 2 * S
 NARROW = S + 32
+HALF = 256
 
 
 def tile_picked_jkeytwicpoddsfrac_none_p_kernel(
@@ -46,18 +47,18 @@ def tile_picked_jkeytwicpoddsfrac_none_p_kernel(
             nc.vector.quantize_mx(out=codes[:].bitcast(FP8X4), scales=scales[:], in_=grouped[:])
             return codes, scales
 
-        def gather(name, dtype, window, offsets):
-            picked = keep.tile([P, S], dtype, name=name, tag=name, align_bytes=64)
+        def gather(name, dtype, window, offsets, tag=None):
+            picked = keep.tile([P, S], dtype, name=name, tag=tag or name, align_bytes=64)
             nc.vector.tensor_copy(picked[:], window.indirect(offsets[:]))
             return picked
 
-        def product(bank, lhs, cols, rhs, start, stop):
+        def product(bank, lhs, cols, rhs, start, stop, places=slice(0, S)):
             nc.tensor.matmul_mx(
-                out=bank[:],
+                out=bank[:, places],
                 lhsT=lhs[0][:, cols].bitcast(FP8X4),
                 lhsT_scale=lhs[1][:, cols],
-                rhs=rhs[0][:].bitcast(FP8X4),
-                rhs_scale=rhs[1][:],
+                rhs=rhs[0][:, places].bitcast(FP8X4),
+                rhs_scale=rhs[1][:, places],
                 start=start,
                 stop=stop,
             )
@@ -66,6 +67,15 @@ def tile_picked_jkeytwicpoddsfrac_none_p_kernel(
             engine_copy(
                 out=grouped[:].rearrange("p (c i t) -> p c t i", i=4, t=PACK),
                 in_=planes[:].rearrange("p t (c i) -> p c t i", i=4),
+            )
+
+        def gain_and_group(grouped, planes, gains, lo, hi):
+            blocks = (hi - lo) // 4
+            nc.vector.tensor_tensor(
+                grouped[:, PACK * lo : PACK * hi].rearrange("p (c i t) -> p c t i", i=4, t=PACK),
+                planes[:, :, lo:hi].rearrange("p t (c i) -> p c t i", i=4),
+                gains[:].unsqueeze(1).unsqueeze(3).to_broadcast([P, blocks, PACK, 4]),
+                ALU.mult,
             )
 
         xs = keep.tile([P, T], U8, name="xs")
@@ -82,13 +92,19 @@ def tile_picked_jkeytwicpoddsfrac_none_p_kernel(
         offs_t = load_list("offs_t", offs)
         for r in range(4):
             nc.sync.dma_start(out=xs[r:P:32, :].bitcast(I32), in_=x_scales[0, r:16:4, :].bitcast(I32))
+        w1_rows = w1.rearrange("(p j) n -> p j n", j=PACK)
+        w1_raw = []
         xw = keep.tile([P, T], I32, name="xw")
-        nc.sync.dma_start(out=xw[:], in_=x_words[0].rearrange("p n t -> p (n t)").bitcast(I32))
-        w1_raw = load_weight("w1_raw", "xt_w", w1)
+        for half, tag in enumerate(("w1_raw0", "xt_w")):
+            raw = keep.tile([P, PACK, HALF], F32, name="w1_raw%d" % half, tag=tag, align_bytes=64)
+            nc.sync.dma_start(out=raw[:], in_=w1_rows[:, :, HALF * half : HALF * (half + 1)])
+            w1_raw.append(raw)
+            if half == 0:
+                nc.sync.dma_start(out=xw[:], in_=x_words[0].rearrange("p n t -> p (n t)").bitcast(I32))
+        two_t = load_list("two_t", two)
         kidx_t = load_list("kidx_t", kidx)
         for e in range(2):
             nc.sync.dma_start(out=ds[e:P:16, :].bitcast(I32), in_=d_scales[0, e:16:2, :].bitcast(I32))
-        two_t = load_list("two_t", two)
         dw = keep.tile([P, G], I32, name="dw", tag="dw", align_bytes=64)
         nc.sync.dma_start(out=dw[:], in_=d_words[0].rearrange("p n t -> p (n t)").bitcast(I32))
         n1_t = load_list("n1_t", n1)
@@ -100,22 +116,23 @@ def tile_picked_jkeytwicpoddsfrac_none_p_kernel(
 
         xo_s = gather("xo_s", U8, xs[:], offs_t)
         xo_w = gather("xo_w", U32, xw[:].bitcast(U32), offs_t)
+        xt_s = gather("xt_s", U8, xs[:], two_t)
         w1_b = keep.tile([P, 2048], BF16, name="w1_b", tag="dk_w", align_bytes=64)
-        nc.scalar.copy(
-            out=w1_b[:].rearrange("p (t m j) -> p m j t", t=PACK, j=PACK),
-            in_=w1_raw[:].rearrange("p j (m t) -> p m j t", t=PACK),
-        )
+        w1_dealt = w1_b[:].rearrange("p (t m j) -> p m j t", t=PACK, j=PACK)
+        for half in range(2):
+            nc.scalar.copy(
+                out=w1_dealt[:, 64 * half : 64 * (half + 1)],
+                in_=w1_raw[half][:].rearrange("p j (m t) -> p m j t", t=PACK),
+            )
         w1_q = quantize("w1", w1_b)
-        dk_s = gather("dk_s", U8, ds[:], kidx_t)
-        dealt_s = keep.tile([P, S], U8, name="dealt_s")
+        dk_s = gather("dk_s", U8, ds[:], kidx_t, "dk_w")
+        dealt_s = keep.tile([P, S], U8, name="dealt_s", tag="dealt_s", align_bytes=64)
         nc.vector.tensor_copy(
             out=dealt_s[:].rearrange("p (t m) -> p t m", t=PACK), in_=dk_s[:].rearrange("p (m t) -> p t m", t=PACK)
         )
         for r in range(4):
             src = 16 * (r // 2) + r % 2
             nc.sync.dma_start(out=dd_s[r:P:32, :].bitcast(I32), in_=dealt_s[src:P:32, :].bitcast(I32))
-        w3_raw = load_weight("w3_raw", "dk_s", w3)
-        xt_s = gather("xt_s", U8, xs[:], two_t)
         xt_w = gather("xt_w", U32, xw[:].bitcast(U32), two_t)
         dk_w = gather("dk_w", U32, dw[:].bitcast(U32), kidx_t)
         dd_w = keep.tile([P, S], U32, name="dd_w", tag="dd_w", align_bytes=64)
@@ -123,6 +140,7 @@ def tile_picked_jkeytwicpoddsfrac_none_p_kernel(
             out=dd_w[:].rearrange("p (t m) -> p t m", t=PACK), in_=dk_w[:].rearrange("p (m t) -> p t m", t=PACK)
         )
         w2_raw = load_weight("w2_raw", "dw", w2)
+        w3_raw = load_weight("w3_raw", "dealt_s", w3)
 
         y_ps = [psum.tile([P, S], F32, name="y_ps%d" % t, tag="bank%d" % t) for t in range(PACK)]
         for t in range(PACK):
@@ -133,24 +151,29 @@ def tile_picked_jkeytwicpoddsfrac_none_p_kernel(
 
         sg, y, st = tiles("sg", WIDE), tiles("y", S), tiles("st", WIDE)
         ex, ex2, num, g3, den = tiles("ex", NARROW), tiles("exb", S), tiles("num", S), tiles("gth", S), tiles("den", S)
-        z_planes = keep.tile([P, PACK, S], BF16, name="z_planes")
-        z2_planes = keep.tile([P, PACK, S], BF16, name="z2_planes")
+        z_planes = keep.tile([P, PACK, S], F32, name="z_planes")
+        z2_planes = keep.tile([P, PACK, S], F32, name="z2_planes")
 
         for t in range(PACK):
-            nc.scalar.activation(sg[t][:, :S], y_ps[t][:], ACT.Sigmoid)
-            nc.scalar.copy(y[t][:], y_ps[t][:])
-            nc.vector.tensor_tensor(st[t][:, :S], sg[t][:].indirect(n1_t[:]), y[t][:], ALU.mult)
+            if t < 2:
+                nc.scalar.activation(sg[t][:, :S], y_ps[t][:], ACT.Sigmoid)
+                nc.scalar.copy(y[t][:], y_ps[t][:])
+                nc.vector.tensor_tensor(st[t][:, :S], sg[t][:].indirect(n1_t[:]), y[t][:], ALU.mult)
+            else:
+                nc.scalar.copy(sg[t][:, :S], y_ps[t][:])
+                nc.scalar.activation(y[t][:], sg[t][:].indirect(n1_t[:]), ACT.Sigmoid)
+                nc.vector.tensor_tensor(st[t][:, :S], sg[t][:, :S], y[t][:], ALU.mult)
         for t in range(PACK):
             s_ps = psum.tile([P, S], F32, name="s_ps%d" % t, tag="bank%d" % t)
             product(s_ps, (dd_w, dd_s), slice(P * t, P * (t + 1)), (xt_w, xt_s), True, True)
             nc.scalar.activation(ex[t][:, :S], s_ps[:], ACT.Exp, scale=0.03125)
             nc.sync.dma_start(out=ex2[t][:], in_=ex[t][:, :S])
-        w3_b = keep.tile([P, 2048], BF16, name="w3_b", tag="dk_w", align_bytes=64)
-        interleave(nc.vector.tensor_copy, w3_b, w3_raw)
-        for t in range(PACK):
             nc.scalar.activation(g3[t][:], ex[t][:].indirect(n3_t[:]), ACT.Copy)
-        w3_q = quantize("w3", w3_b)
+        w2_b = keep.tile([P, 2048], BF16, name="w2_b", tag="dk_w", align_bytes=64)
+        interleave(nc.vector.tensor_copy, w2_b, w2_raw)
+        w2_q = quantize("w2", w2_b)
         for t in range(PACK):
+            nc.vector.tensor_tensor(den[t][:], ex[t][:].indirect(n4_t[:]), g3[t][:], ALU.add)
             nc.vector.tensor_tensor(num[t][:], ex[t][:].indirect(n2_t[:]), ex2[t][:], ALU.add)
         stg = [
             keep.tile([P, S], F32, name="stg%d" % t, tag=tag, align_bytes=64)
@@ -159,38 +182,49 @@ def tile_picked_jkeytwicpoddsfrac_none_p_kernel(
         for t in range(PACK):
             nc.scalar.activation(stg[t][:], st[t][:].indirect(n1_t[:]), ACT.Copy)
         for t in range(PACK):
-            nc.vector.tensor_tensor(den[t][:], ex[t][:].indirect(n4_t[:]), g3[t][:], ALU.add)
-        for t in range(PACK):
+            nc.scalar.activation(g3[t][:], den[t][:], ACT.Ln)
             nc.scalar.activation(num[t][:], num[t][:], ACT.Ln)
         for t in range(PACK):
-            nc.vector.tensor_tensor(stg[t][:], stg[t][:], st[t][:, :S], ALU.max)
-        for t in range(PACK):
-            nc.scalar.activation(g3[t][:], den[t][:], ACT.Ln)
-            nc.vector.tensor_tensor(num[t][:], num[t][:], g3[t][:], ALU.subtract)
-            nc.vector.tensor_scalar(z2_planes[:, t, :], num[t][:], gk_t[:, t : t + 1], None, ALU.mult)
-        for t in range(PACK):
-            nc.scalar.activation(z_planes[:, t, :], stg[t][:], ACT.Copy, scale=gn_t[:, t : t + 1])
-        z2_b = keep.tile([P, 2048], BF16, name="z2_b", align_bytes=64)
-        interleave(nc.vector.tensor_copy, z2_b, z2_planes)
-        w2_b = keep.tile([P, 2048], BF16, name="w2_b", tag="ex3", align_bytes=64)
-        interleave(nc.scalar.copy, w2_b, w2_raw)
+            nc.vector.tensor_tensor(z_planes[:, t, :], stg[t][:], st[t][:, :S], ALU.max)
         z_b = keep.tile([P, 2048], BF16, name="z_b", align_bytes=64)
-        interleave(nc.vector.tensor_copy, z_b, z_planes)
-        z2_q = quantize("z2", z2_b)
+        gain_and_group(z_b, z_planes, gn_t, 0, S)
+        w3_b = keep.tile([P, 2048], BF16, name="w3_b", tag="ex3", align_bytes=64)
+        interleave(nc.scalar.copy, w3_b, w3_raw)
+        nc.vector.tensor_tensor(z2_planes[:, 0, :], num[0][:], g3[0][:], ALU.subtract)
         z_q = quantize("z", z_b)
-        w2_q = quantize("w2", w2_b)
+        for t in range(1, PACK):
+            nc.vector.tensor_tensor(z2_planes[:, t, :], num[t][:], g3[t][:], ALU.subtract)
+        z2_b = keep.tile([P, 2048], BF16, name="z2_b", align_bytes=64)
+        gain_and_group(z2_b, z2_planes, gk_t, 0, HALF)
+        w3_q = quantize("w3", w3_b)
+        gain_and_group(z2_b, z2_planes, gk_t, HALF, S)
+        z2_codes = keep.tile([P, S], U32, name="z2_codes", align_bytes=64)
+        z2_scales = keep.tile([P, S], U8, name="z2_scales", align_bytes=64)
+        for half in range(2):
+            cols = slice(HALF * half, HALF * (half + 1))
+            nc.vector.quantize_mx(
+                out=z2_codes[:, cols].bitcast(FP8X4),
+                scales=z2_scales[:, cols],
+                in_=z2_b[:, PACK * cols.start : PACK * cols.stop],
+            )
 
         h_ps = [psum.tile([P, S], F32, name="h_ps%d" % m) for m in range(PACK)]
         for m in range(PACK):
-            product(h_ps[m], w3_q, slice(P * m, P * (m + 1)), z2_q, True, False)
-        for m in range(PACK):
-            product(h_ps[m], w2_q, slice(P * m, P * (m + 1)), z_q, False, True)
+            product(h_ps[m], w2_q, slice(P * m, P * (m + 1)), z_q, True, False)
+        for half in range(2):
+            for m in range(PACK):
+                cols = slice(HALF * half, HALF * (half + 1))
+                product(h_ps[m], w3_q, slice(P * m, P * (m + 1)), (z2_codes, z2_scales), False, half == 1, cols)
 
-        h, h2, d6 = tiles("h", WIDE), tiles("hb", S), tiles("dsix", S)
-        d5 = [h[(m - 1) % PACK][:, S:] for m in range(PACK)]
+        h2, d6 = tiles("hb", S), tiles("dsix", S)
+        h = [keep.tile([P, WIDE * (2 if m == PACK - 1 else 1)], F32, name="h%d" % m) for m in range(PACK)]
+        d5 = [h[PACK - 1][:, S * (m + 1) : S * (m + 2)] for m in range(PACK - 1)] + [h[0][:, S:]]
         for m in range(PACK):
-            nc.scalar.copy(h[m][:, :S], h_ps[m][:])
-            if m in (0, PACK - 1):
+            if m == 1:
+                nc.vector.tensor_copy(h[m][:, :S], h_ps[m][:])
+            else:
+                nc.scalar.copy(h[m][:, :S], h_ps[m][:])
+            if m == 0:
                 nc.vector.tensor_copy(h2[m][:], h[m][:, :S])
             else:
                 nc.scalar.copy(h2[m][:], h_ps[m][:])

@@ -41,8 +41,8 @@ def tile_picked_jkeytwicpoddsfrac_none_p_kernel(
             nc.sync.dma_start(out=raw[:], in_=w.rearrange("(p j) n -> p j n", j=PACK))
             return raw
 
-        def quantize(name, grouped):
-            codes = keep.tile([P, 512], U32, name=name + "_codes", align_bytes=64)
+        def quantize(name, grouped, tag=None):
+            codes = keep.tile([P, 512], U32, name=name + "_codes", tag=tag or name + "_codes", align_bytes=64)
             scales = keep.tile([P, 512], U8, name=name + "_scales", align_bytes=64)
             nc.vector.quantize_mx(out=codes[:].bitcast(FP8X4), scales=scales[:], in_=grouped[:])
             return codes, scales
@@ -72,7 +72,7 @@ def tile_picked_jkeytwicpoddsfrac_none_p_kernel(
         def gain_and_group(grouped, planes, gains, lo, hi):
             blocks = (hi - lo) // 4
             nc.vector.tensor_tensor(
-                grouped[:, PACK * lo : PACK * hi].rearrange("p (c i t) -> p c t i", i=4, t=PACK),
+                grouped[:].rearrange("p (c i t) -> p c t i", i=4, t=PACK),
                 planes[:, :, lo:hi].rearrange("p t (c i) -> p c t i", i=4),
                 gains[:].unsqueeze(1).unsqueeze(3).to_broadcast([P, blocks, PACK, 4]),
                 ALU.mult,
@@ -80,44 +80,41 @@ def tile_picked_jkeytwicpoddsfrac_none_p_kernel(
 
         xs = keep.tile([P, T], U8, name="xs")
         ds = keep.tile([P, G], U8, name="ds")
-        dd_s = keep.tile([P, S], U8, name="dd_s", tag="dd_s", align_bytes=64)
         nc.gpsimd.memset(xs[:].bitcast(I32), 0)
         nc.gpsimd.memset(ds[:].bitcast(I32), 0)
-        nc.gpsimd.memset(dd_s[:].bitcast(I32), 0)
         gn_t = keep.tile([P, PACK], F32, name="gn_t")
         gk_t = keep.tile([P, PACK], F32, name="gk_t")
-        nc.gpsimd.dma_start(out=gk_t[:], in_=gk.rearrange("(p t) o -> p (t o)", t=PACK))
         nc.gpsimd.dma_start(out=gn_t[:], in_=gn.rearrange("(p t) o -> p (t o)", t=PACK))
+        nc.gpsimd.dma_start(out=gk_t[:], in_=gk.rearrange("(p t) o -> p (t o)", t=PACK))
 
         offs_t = load_list("offs_t", offs)
         for r in range(4):
             nc.sync.dma_start(out=xs[r:P:32, :].bitcast(I32), in_=x_scales[0, r:16:4, :].bitcast(I32))
-        w1_rows = w1.rearrange("(p j) n -> p j n", j=PACK)
-        w1_raw = []
-        xw = keep.tile([P, T], I32, name="xw")
-        for half, tag in enumerate(("w1_raw0", "xt_w")):
-            raw = keep.tile([P, PACK, HALF], F32, name="w1_raw%d" % half, tag=tag, align_bytes=64)
-            nc.sync.dma_start(out=raw[:], in_=w1_rows[:, :, HALF * half : HALF * (half + 1)])
-            w1_raw.append(raw)
-            if half == 0:
-                nc.sync.dma_start(out=xw[:], in_=x_words[0].rearrange("p n t -> p (n t)").bitcast(I32))
         two_t = load_list("two_t", two)
+        w1_rows = w1.rearrange("(p j) n -> p j n", j=PACK)
+        w1_raw = [keep.tile([P, PACK, HALF], F32, name="w1_raw%d" % half, tag="w1_raw%d" % half, align_bytes=64) for half in range(2)]
+        xw = keep.tile([P, T], I32, name="xw")
+        nc.sync.dma_start(out=w1_raw[0][:], in_=w1_rows[:, :, :HALF])
+        nc.sync.dma_start(out=xw[:], in_=x_words[0].rearrange("p n t -> p (n t)").bitcast(I32))
         kidx_t = load_list("kidx_t", kidx)
         for e in range(2):
             nc.sync.dma_start(out=ds[e:P:16, :].bitcast(I32), in_=d_scales[0, e:16:2, :].bitcast(I32))
-        dw = keep.tile([P, G], I32, name="dw", tag="dw", align_bytes=64)
+        nc.sync.dma_start(out=w1_raw[1][:], in_=w1_rows[:, :, HALF:])
+        dw = keep.tile([P, G], I32, name="dw")
         nc.sync.dma_start(out=dw[:], in_=d_words[0].rearrange("p n t -> p (n t)").bitcast(I32))
         n1_t = load_list("n1_t", n1)
         n3_t = load_list("n3_t", n3)
-        n2_t = load_list("n2_t", n2)
+        w2_raw = load_weight("w2_raw", "w2_raw", w2)
         n4_t = load_list("n4_t", n4)
+        n2_t = load_list("n2_t", n2)
         n6_t = load_list("n6_t", n6)
         n5_t = load_list("n5_t", n5)
 
         xo_s = gather("xo_s", U8, xs[:], offs_t)
-        xo_w = gather("xo_w", U32, xw[:].bitcast(U32), offs_t)
         xt_s = gather("xt_s", U8, xs[:], two_t)
-        w1_b = keep.tile([P, 2048], BF16, name="w1_b", tag="dk_w", align_bytes=64)
+        xo_w = gather("xo_w", U32, xw[:].bitcast(U32), offs_t)
+        dk_s = gather("dk_s", U8, ds[:], kidx_t)
+        w1_b = keep.tile([P, 2048], BF16, name="w1_b", align_bytes=64)
         w1_dealt = w1_b[:].rearrange("p (t m j) -> p m j t", t=PACK, j=PACK)
         for half in range(2):
             nc.scalar.copy(
@@ -125,22 +122,21 @@ def tile_picked_jkeytwicpoddsfrac_none_p_kernel(
                 in_=w1_raw[half][:].rearrange("p j (m t) -> p m j t", t=PACK),
             )
         w1_q = quantize("w1", w1_b)
-        dk_s = gather("dk_s", U8, ds[:], kidx_t, "dk_w")
-        dealt_s = keep.tile([P, S], U8, name="dealt_s", tag="dealt_s", align_bytes=64)
+        dd_s = keep.tile([P, S], U8, name="dd_s", tag="dd_s", align_bytes=64)
         nc.vector.tensor_copy(
-            out=dealt_s[:].rearrange("p (t m) -> p t m", t=PACK), in_=dk_s[:].rearrange("p (m t) -> p t m", t=PACK)
+            out=dd_s[:].rearrange("p (t m) -> p t m", t=PACK), in_=dk_s[:].rearrange("p (m t) -> p t m", t=PACK)
         )
-        for r in range(4):
-            src = 16 * (r // 2) + r % 2
-            nc.sync.dma_start(out=dd_s[r:P:32, :].bitcast(I32), in_=dealt_s[src:P:32, :].bitcast(I32))
-        xt_w = gather("xt_w", U32, xw[:].bitcast(U32), two_t)
+        for e in range(2):
+            nc.sync.dma_start(out=dd_s[2 + e : P : 32, :].bitcast(I32), in_=dd_s[16 + e : P : 32, :].bitcast(I32))
+        w3_raw = load_weight("w3_raw", "dk_s", w3)
         dk_w = gather("dk_w", U32, dw[:].bitcast(U32), kidx_t)
+        xt_w = gather("xt_w", U32, xw[:].bitcast(U32), two_t, "w1_raw1")
         dd_w = keep.tile([P, S], U32, name="dd_w", tag="dd_w", align_bytes=64)
         nc.vector.tensor_copy(
             out=dd_w[:].rearrange("p (t m) -> p t m", t=PACK), in_=dk_w[:].rearrange("p (m t) -> p t m", t=PACK)
         )
-        w2_raw = load_weight("w2_raw", "dw", w2)
-        w3_raw = load_weight("w3_raw", "dealt_s", w3)
+        w2_b = keep.tile([P, 2048], BF16, name="w2_b", align_bytes=64)
+        interleave(nc.vector.tensor_copy, w2_b, w2_raw)
 
         y_ps = [psum.tile([P, S], F32, name="y_ps%d" % t, tag="bank%d" % t) for t in range(PACK)]
         for t in range(PACK):
@@ -149,66 +145,94 @@ def tile_picked_jkeytwicpoddsfrac_none_p_kernel(
         def tiles(name, width, dtype=F32):
             return [keep.tile([P, width], dtype, name="%s%d" % (name, t), tag="%s%d" % (name, t), align_bytes=64) for t in range(PACK)]
 
-        sg, y, st = tiles("sg", WIDE), tiles("y", S), tiles("st", WIDE)
-        ex, ex2, num, g3, den = tiles("ex", NARROW), tiles("exb", S), tiles("num", S), tiles("gth", S), tiles("den", S)
-        z_planes = keep.tile([P, PACK, S], F32, name="z_planes")
-        z2_planes = keep.tile([P, PACK, S], F32, name="z2_planes")
+        th, ex, g3 = tiles("th", WIDE), tiles("ex", WIDE), tiles("gth", S)
+        st = [None] * PACK
+        num = keep.tile([P, PACK, S], F32, name="num")
 
+        def held(name, tags):
+            return [keep.tile([P, S], F32, name="%s%d" % (name, t), tag=tag, align_bytes=64) for t, tag in enumerate(tags)]
+
+        def gate(t):
+            nc.scalar.activation(sg[t][:], th[t][:].indirect(n1_t[:]), ACT.Copy, bias=0.5, scale=0.5)
+
+        def gated(t):
+            st[t] = keep.tile([P, WIDE], F32, name="st%d" % t, tag=("w2_raw", "ex1", "gth2", "ex2")[t], align_bytes=64)
+            nc.vector.tensor_tensor(st[t][:, :S], sg[t][:], y_ps[t][:], ALU.mult)
+
+        sg = held("sg", ("sg0",))
         for t in range(PACK):
-            if t < 2:
-                nc.scalar.activation(sg[t][:, :S], y_ps[t][:], ACT.Sigmoid)
-                nc.scalar.copy(y[t][:], y_ps[t][:])
-                nc.vector.tensor_tensor(st[t][:, :S], sg[t][:].indirect(n1_t[:]), y[t][:], ALU.mult)
-            else:
-                nc.scalar.copy(sg[t][:, :S], y_ps[t][:])
-                nc.scalar.activation(y[t][:], sg[t][:].indirect(n1_t[:]), ACT.Sigmoid)
-                nc.vector.tensor_tensor(st[t][:, :S], sg[t][:, :S], y[t][:], ALU.mult)
-        for t in range(PACK):
-            s_ps = psum.tile([P, S], F32, name="s_ps%d" % t, tag="bank%d" % t)
-            product(s_ps, (dd_w, dd_s), slice(P * t, P * (t + 1)), (xt_w, xt_s), True, True)
-            nc.scalar.activation(ex[t][:, :S], s_ps[:], ACT.Exp, scale=0.03125)
-            nc.sync.dma_start(out=ex2[t][:], in_=ex[t][:, :S])
-            nc.scalar.activation(g3[t][:], ex[t][:].indirect(n3_t[:]), ACT.Copy)
-        w2_b = keep.tile([P, 2048], BF16, name="w2_b", tag="dk_w", align_bytes=64)
-        interleave(nc.vector.tensor_copy, w2_b, w2_raw)
+            nc.scalar.activation(th[t][:, :S], y_ps[t][:], ACT.Tanh, scale=0.5)
+        gate(0)
+        gated(0)
         w2_q = quantize("w2", w2_b)
-        for t in range(PACK):
-            nc.vector.tensor_tensor(den[t][:], ex[t][:].indirect(n4_t[:]), g3[t][:], ALU.add)
-            nc.vector.tensor_tensor(num[t][:], ex[t][:].indirect(n2_t[:]), ex2[t][:], ALU.add)
-        stg = [
-            keep.tile([P, S], F32, name="stg%d" % t, tag=tag, align_bytes=64)
-            for t, tag in enumerate(("xt_w", "dd_w", "xt_s", "dd_s"))
-        ]
+        w3_b = keep.tile([P, 2048], BF16, name="w3_b", align_bytes=64)
+        interleave(nc.vector.tensor_copy, w3_b, w3_raw)
+        rows = keep.tile([P, PACK + 2, S], F32, name="rows", tag="dk_s", align_bytes=64)
+        den = rows[:, :PACK, :]
+        ex2 = [rows[:, slot, :] for slot in (4, 2, 3, 5)]
+        s_ps = [psum.tile([P, S], F32, name="s_ps%d" % t, tag="bank%d" % (PACK + t)) for t in range(PACK)]
+        for t in range(PACK + 1):
+            if t < PACK:
+                product(s_ps[t], (dd_w, dd_s), slice(P * t, P * (t + 1)), (xt_w, xt_s), True, True)
+                nc.scalar.activation(ex[t][:, :S], s_ps[t][:], ACT.Exp, scale=0.03125)
+                nc.sync.dma_start(out=ex2[t], in_=ex[t][:, :S])
+            if t > 0:
+                nc.scalar.activation(g3[t - 1][:], ex[t - 1][:].indirect(n3_t[:]), ACT.Copy)
+        sg.extend(held("late_sg", ("w1_raw1", "dd_w", "xt_s")))
+        for t in range(1, PACK):
+            gate(t)
+
+        def denominator(t):
+            nc.vector.tensor_tensor(den[:, t, :], ex[t][:].indirect(n4_t[:]), g3[t][:], ALU.add)
+
+        def numerator(t):
+            nc.vector.tensor_tensor(num[:, t, :], ex[t][:].indirect(n2_t[:]), ex2[t], ALU.add)
+
+        denominator(0)
+        w3_q = quantize("w3", w3_b)
+        denominator(1)
+        numerator(0)
+        numerator(1)
+        denominator(2)
+        gated(1)
+        gated(2)
+        numerator(2)
+        gated(3)
+        denominator(3)
+        numerator(3)
+        stg = held("stg", ("dd_s", "stg1", "stg2", "stg3"))
         for t in range(PACK):
             nc.scalar.activation(stg[t][:], st[t][:].indirect(n1_t[:]), ACT.Copy)
-        for t in range(PACK):
-            nc.scalar.activation(g3[t][:], den[t][:], ACT.Ln)
-            nc.scalar.activation(num[t][:], num[t][:], ACT.Ln)
+        halves = [slice(HALF * half, HALF * (half + 1)) for half in range(2)]
+        for cols in halves:
+            nc.scalar.activation(den[:, :, cols], den[:, :, cols], ACT.Ln)
+            nc.scalar.activation(num[:, :, cols], num[:, :, cols], ACT.Ln)
+        z_planes = keep.tile([P, PACK, S], F32, name="z_planes", tag="ex3", align_bytes=64)
         for t in range(PACK):
             nc.vector.tensor_tensor(z_planes[:, t, :], stg[t][:], st[t][:, :S], ALU.max)
         z_b = keep.tile([P, 2048], BF16, name="z_b", align_bytes=64)
         gain_and_group(z_b, z_planes, gn_t, 0, S)
-        w3_b = keep.tile([P, 2048], BF16, name="w3_b", tag="ex3", align_bytes=64)
-        interleave(nc.scalar.copy, w3_b, w3_raw)
-        nc.vector.tensor_tensor(z2_planes[:, 0, :], num[0][:], g3[0][:], ALU.subtract)
-        z_q = quantize("z", z_b)
-        for t in range(1, PACK):
-            nc.vector.tensor_tensor(z2_planes[:, t, :], num[t][:], g3[t][:], ALU.subtract)
-        z2_b = keep.tile([P, 2048], BF16, name="z2_b", align_bytes=64)
-        gain_and_group(z2_b, z2_planes, gk_t, 0, HALF)
-        w3_q = quantize("w3", w3_b)
-        gain_and_group(z2_b, z2_planes, gk_t, HALF, S)
         z2_codes = keep.tile([P, S], U32, name="z2_codes", align_bytes=64)
         z2_scales = keep.tile([P, S], U8, name="z2_scales", align_bytes=64)
-        for half in range(2):
-            cols = slice(HALF * half, HALF * (half + 1))
+
+        def quantize_z2(cols, grouped):
             nc.vector.quantize_mx(
                 out=z2_codes[:, cols].bitcast(FP8X4),
                 scales=z2_scales[:, cols],
-                in_=z2_b[:, PACK * cols.start : PACK * cols.stop],
+                in_=grouped[:],
             )
 
-        h_ps = [psum.tile([P, S], F32, name="h_ps%d" % m) for m in range(PACK)]
+        z2_lo = keep.tile([P, PACK * HALF], BF16, name="z2_lo", align_bytes=64)
+        z2_hi = keep.tile([P, PACK * HALF], BF16, name="z2_hi", align_bytes=64)
+        nc.vector.tensor_tensor(num[:, :, halves[0]], num[:, :, halves[0]], den[:, :, halves[0]], ALU.subtract)
+        z_q = quantize("z", z_b)
+        gain_and_group(z2_lo, num, gk_t, 0, HALF)
+        nc.vector.tensor_tensor(num[:, :, halves[1]], num[:, :, halves[1]], den[:, :, halves[1]], ALU.subtract)
+        quantize_z2(halves[0], z2_lo)
+        gain_and_group(z2_hi, num, gk_t, HALF, S)
+        quantize_z2(halves[1], z2_hi)
+
+        h_ps = [psum.tile([P, S], F32, name="h_ps%d" % m, tag="bank%d" % (PACK + m)) for m in range(PACK)]
         for m in range(PACK):
             product(h_ps[m], w2_q, slice(P * m, P * (m + 1)), z_q, True, False)
         for half in range(2):
@@ -216,25 +240,51 @@ def tile_picked_jkeytwicpoddsfrac_none_p_kernel(
                 cols = slice(HALF * half, HALF * (half + 1))
                 product(h_ps[m], w3_q, slice(P * m, P * (m + 1)), (z2_codes, z2_scales), False, half == 1, cols)
 
-        h2, d6 = tiles("hb", S), tiles("dsix", S)
+        h2, d6, root = tiles("hb", S), tiles("dsix", S), tiles("root", S)
         h = [keep.tile([P, WIDE * (2 if m == PACK - 1 else 1)], F32, name="h%d" % m) for m in range(PACK)]
-        d5 = [h[PACK - 1][:, S * (m + 1) : S * (m + 2)] for m in range(PACK - 1)] + [h[0][:, S:]]
+        fetched = keep.tile([P, S], F32, name="fetched")
+        first = keep.tile([P, S], F32, name="first")
+        d5 = [first[:], h[3][:, S : 2 * S], fetched[:], h[0][:, S:]]
+        result = [h[3][:, 2 * S : 3 * S]] + [h2[m][:] for m in range(1, PACK)]
         for m in range(PACK):
             if m == 1:
-                nc.vector.tensor_copy(h[m][:, :S], h_ps[m][:])
-            else:
-                nc.scalar.copy(h[m][:, :S], h_ps[m][:])
-            if m == 0:
-                nc.vector.tensor_copy(h2[m][:], h[m][:, :S])
-            else:
-                nc.scalar.copy(h2[m][:], h_ps[m][:])
-            nc.vector.tensor_tensor(d6[m][:], h[m][:].indirect(n6_t[:]), h2[m][:], ALU.subtract)
+                nc.vector.tensor_copy(h2[m][:], h_ps[m][:])
+            nc.scalar.copy(h[m][:, :S], h_ps[m][:])
+            if m == 1:
+                nc.vector.tensor_copy(h2[0][:], h[0][:, :S])
+            elif m > 1:
+                nc.sync.dma_start(out=h2[m][:], in_=h[m][:, :S])
+
+        def minus_h(dst, m, places):
+            nc.vector.tensor_tensor(dst, h[m][:].indirect(places[:]), h2[m][:], ALU.subtract)
+
+        def size(m):
+            nc.scalar.activation(root[m][:], d6[m][:], ACT.Abs)
+
+        def inverse_root(m):
+            nc.scalar.activation(root[m][:], root[m][:], ACT.Abs_reciprocal_sqrt, bias=0.5)
+
+        def inverse(m):
+            nc.scalar.activation(d6[(m + 1) % PACK][:], root[m][:], ACT.Square)
+
+        def store(m):
+            nc.vector.scalar_tensor_tensor(result[m], d5[m], -1.0, d6[(m + 1) % PACK][:], ALU.mult, ALU.mult)
+            nc.sync.dma_start(out=out[P * m : P * (m + 1), :], in_=result[m])
+
+        nc.scalar.activation(d5[2], h[2][:].indirect(n5_t[:]), ACT.Copy)
         for m in range(PACK):
-            nc.scalar.activation(d6[m][:], d6[m][:], ACT.Abs)
-            nc.scalar.activation(d6[m][:], d6[m][:], ACT.Ln, bias=0.5)
+            minus_h(d6[m][:], m, n6_t)
+            if m == 1:
+                minus_h(d5[0], 0, n5_t)
+        size(0)
         for m in range(PACK):
-            nc.vector.tensor_tensor(d5[m], h[m][:].indirect(n5_t[:]), h2[m][:], ALU.subtract)
-        for m in range(PACK):
-            nc.scalar.activation(d6[m][:], d6[m][:], ACT.Exp, scale=-1.0)
-            nc.vector.scalar_tensor_tensor(h2[m][:], d5[m], -1.0, d6[m][:], ALU.mult, ALU.mult)
-            nc.sync.dma_start(out=out[P * m : P * (m + 1), :], in_=h2[m][:])
+            inverse_root(m)
+            if m + 1 < PACK:
+                size(m + 1)
+            inverse(m)
+        minus_h(d5[1], 1, n5_t)
+        store(0)
+        nc.vector.tensor_tensor(d5[2], d5[2], h2[2][:], ALU.subtract)
+        minus_h(d5[3], 3, n5_t)
+        for m in range(1, PACK):
+            store(m)

@@ -207,6 +207,8 @@ def tile_picked_jkeytwicpoddsfrac_none_p_kernel(
         for cols in halves:
             nc.scalar.activation(den[:, :, cols], den[:, :, cols], ACT.Ln)
             nc.scalar.activation(num[:, :, cols], num[:, :, cols], ACT.Ln)
+        warm = keep.tile([P, 8], F32, name="warm")
+        nc.scalar.activation(warm[:, 0:1], den[:, PACK - 1, S - 1 : S], ACT.Abs_reciprocal_sqrt, bias=0.5)
         z_planes = keep.tile([P, PACK, S], F32, name="z_planes", tag="ex3", align_bytes=64)
         for t in range(PACK):
             nc.vector.tensor_tensor(z_planes[:, t, :], stg[t][:], st[t][:, :S], ALU.max)
@@ -242,49 +244,37 @@ def tile_picked_jkeytwicpoddsfrac_none_p_kernel(
 
         h2, d6, root = tiles("hb", S), tiles("dsix", S), tiles("root", S)
         h = [keep.tile([P, WIDE * (2 if m == PACK - 1 else 1)], F32, name="h%d" % m) for m in range(PACK)]
-        fetched = keep.tile([P, S], F32, name="fetched")
-        first = keep.tile([P, S], F32, name="first")
-        d5 = [first[:], h[3][:, S : 2 * S], fetched[:], h[0][:, S:]]
-        result = [h[3][:, 2 * S : 3 * S]] + [h2[m][:] for m in range(1, PACK)]
-        for m in range(PACK):
-            if m == 1:
-                nc.vector.tensor_copy(h2[m][:], h_ps[m][:])
+        spare = [h[3][:, S * (i + 1) : S * (i + 2)] for i in range(3)]
+        fetched = tiles("fetched", S)
+        d5 = [fetched[0][:], spare[0], fetched[2][:], fetched[3][:]]
+        result = [spare[1]] + [h2[m][:] for m in range(1, PACK)]
+        inverse_root = [root[0][:], root[1][:], spare[2], root[3][:]]
+        nc.vector.tensor_copy(h2[1][:], h_ps[1][:])
+        for m in (0, 2, 3, 1):
             nc.scalar.copy(h[m][:, :S], h_ps[m][:])
-            if m == 1:
-                nc.vector.tensor_copy(h2[0][:], h[0][:, :S])
-            elif m > 1:
+            if m > 1:
                 nc.sync.dma_start(out=h2[m][:], in_=h[m][:, :S])
+        nc.vector.tensor_copy(h2[0][:], h[0][:, :S])
 
         def minus_h(dst, m, places):
             nc.vector.tensor_tensor(dst, h[m][:].indirect(places[:]), h2[m][:], ALU.subtract)
 
-        def size(m):
-            nc.scalar.activation(root[m][:], d6[m][:], ACT.Abs)
-
-        def inverse_root(m):
-            nc.scalar.activation(root[m][:], root[m][:], ACT.Abs_reciprocal_sqrt, bias=0.5)
-
-        def inverse(m):
-            nc.scalar.activation(d6[(m + 1) % PACK][:], root[m][:], ACT.Square)
-
-        def store(m):
-            nc.vector.scalar_tensor_tensor(result[m], d5[m], -1.0, d6[(m + 1) % PACK][:], ALU.mult, ALU.mult)
-            nc.sync.dma_start(out=out[P * m : P * (m + 1), :], in_=result[m])
-
-        nc.scalar.activation(d5[2], h[2][:].indirect(n5_t[:]), ACT.Copy)
+        for m in (2, 3):
+            nc.scalar.activation(d5[m], h[m][:].indirect(n5_t[:]), ACT.Copy)
         for m in range(PACK):
             minus_h(d6[m][:], m, n6_t)
             if m == 1:
                 minus_h(d5[0], 0, n5_t)
-        size(0)
-        for m in range(PACK):
-            inverse_root(m)
-            if m + 1 < PACK:
-                size(m + 1)
-            inverse(m)
+        for pair in ((0, 1), (2, 3)):
+            for m in pair:
+                nc.scalar.activation(d6[m][:], d6[m][:], ACT.Abs)
+            for m in pair:
+                nc.scalar.activation(inverse_root[m], d6[m][:], ACT.Abs_reciprocal_sqrt, bias=0.5)
+            for m in pair:
+                nc.scalar.activation(d6[m][:], inverse_root[m], ACT.Square)
         minus_h(d5[1], 1, n5_t)
-        store(0)
-        nc.vector.tensor_tensor(d5[2], d5[2], h2[2][:], ALU.subtract)
-        minus_h(d5[3], 3, n5_t)
-        for m in range(1, PACK):
-            store(m)
+        for m in (2, 3):
+            nc.vector.tensor_tensor(d5[m], d5[m], h2[m][:], ALU.subtract)
+        for m in range(PACK):
+            nc.vector.scalar_tensor_tensor(result[m], d5[m], -1.0, d6[m][:], ALU.mult, ALU.mult)
+            nc.sync.dma_start(out=out[P * m : P * (m + 1), :], in_=result[m])

from contextlib import ExitStack

import concourse.mybir as mybir

K, T, S, N, H, G = 512, 1024, 512, 512, 512, 2048
FLOPS = 4 * 2 * 512 * 512 * 512

F32 = mybir.dt.float32
BF16 = mybir.dt.bfloat16
I32 = mybir.dt.int32
U32 = mybir.dt.uint32
U16 = mybir.dt.uint16
U8 = mybir.dt.uint8
FP8X4 = mybir.dt.float8_e4m3fn_x4
ALU = mybir.AluOpType
ACT = mybir.ActivationFunctionType

P = 128
PACK = 4
WIDE = 2 * S
NARROW = S + 32
HALF = 256


def tile_picked_jkeytwicpoddsfrac_none_p_kernel(
    tc, x_words, x_scales, w1, d_words, d_scales, gn, gk, w2, w3, offs, kidx, two, n1, n2, n3, n4, n5, n6, out
):
    nc = tc.nc
    with ExitStack() as ctx:
        lists = ctx.enter_context(tc.tile_pool(name="lists", bufs=1))
        keep = ctx.enter_context(tc.tile_pool(name="keep", bufs=1))
        psum = ctx.enter_context(tc.psum_pool(name="psum", bufs=1))

        def load_list(name, src):
            tile = lists.tile([P, S // 16], U16, name=name)
            nc.sync.dma_start(tile[:], src)
            return tile

        def load_weight(name, tag, w):
            raw = keep.tile([P, PACK, 512], F32, name=name, tag=tag, align_bytes=64)
            nc.sync.dma_start(out=raw[:], in_=w.rearrange("(p j) n -> p j n", j=PACK))
            return raw

        def quantize(name, grouped, tag=None):
            codes = keep.tile([P, 512], U32, name=name + "_codes", tag=tag or name + "_codes", align_bytes=64)
            scales = keep.tile([P, 512], U8, name=name + "_scales", align_bytes=64)
            nc.vector.quantize_mx(out=codes[:].bitcast(FP8X4), scales=scales[:], in_=grouped[:])
            return codes, scales

        def gather(name, dtype, window, offsets, tag=None):
            picked = keep.tile([P, S], dtype, name=name, tag=tag or name, align_bytes=64)
            nc.vector.tensor_copy(picked[:], window.indirect(offsets[:]))
            return picked

        def product(bank, lhs, cols, rhs, start, stop, places=slice(0, S)):
            nc.tensor.matmul_mx(
                out=bank[:, places],
                lhsT=lhs[0][:, cols].bitcast(FP8X4),
                lhsT_scale=lhs[1][:, cols],
                rhs=rhs[0][:, places].bitcast(FP8X4),
                rhs_scale=rhs[1][:, places],
                start=start,
                stop=stop,
            )

        def interleave(engine_copy, grouped, planes):
            engine_copy(
                out=grouped[:].rearrange("p (c i t) -> p c t i", i=4, t=PACK),
                in_=planes[:].rearrange("p t (c i) -> p c t i", i=4),
            )

        def gain_and_group(grouped, planes, gains, lo, hi):
            blocks = (hi - lo) // 4
            nc.vector.tensor_tensor(
                grouped[:].rearrange("p (c i t) -> p c t i", i=4, t=PACK),
                planes[:, :, lo:hi].rearrange("p t (c i) -> p c t i", i=4),
                gains[:].unsqueeze(1).unsqueeze(3).to_broadcast([P, blocks, PACK, 4]),
                ALU.mult,
            )

        xs = keep.tile([P, T], U8, name="xs")
        ds = keep.tile([P, G], U8, name="ds")
        nc.gpsimd.memset(xs[:].bitcast(I32), 0)
        nc.gpsimd.memset(ds[:].bitcast(I32), 0)
        gn_t = keep.tile([P, PACK], F32, name="gn_t")
        gk_t = keep.tile([P, PACK], F32, name="gk_t")
        nc.gpsimd.dma_start(out=gn_t[:], in_=gn.rearrange("(p t) o -> p (t o)", t=PACK))
        nc.gpsimd.dma_start(out=gk_t[:], in_=gk.rearrange("(p t) o -> p (t o)", t=PACK))

        offs_t = load_list("offs_t", offs)
        for r in range(4):
            nc.sync.dma_start(out=xs[r:P:32, :].bitcast(I32), in_=x_scales[0, r:16:4, :].bitcast(I32))
        two_t = load_list("two_t", two)
        w1_rows = w1.rearrange("(p j) n -> p j n", j=PACK)
        w1_raw = [keep.tile([P, PACK, HALF], F32, name="w1_raw%d" % half, tag="w1_raw%d" % half, align_bytes=64) for half in range(2)]
        xw = keep.tile([P, T], I32, name="xw")
        nc.sync.dma_start(out=w1_raw[0][:], in_=w1_rows[:, :, :HALF])
        nc.sync.dma_start(out=xw[:], in_=x_words[0].rearrange("p n t -> p (n t)").bitcast(I32))
        kidx_t = load_list("kidx_t", kidx)
        for e in range(2):
            nc.sync.dma_start(out=ds[e:P:16, :].bitcast(I32), in_=d_scales[0, e:16:2, :].bitcast(I32))
        nc.sync.dma_start(out=w1_raw[1][:], in_=w1_rows[:, :, HALF:])
        dw = keep.tile([P, G], I32, name="dw")
        nc.sync.dma_start(out=dw[:], in_=d_words[0].rearrange("p n t -> p (n t)").bitcast(I32))
        n1_t = load_list("n1_t", n1)
        n3_t = load_list("n3_t", n3)
        w2_raw = load_weight("w2_raw", "w2_raw", w2)
        n4_t = load_list("n4_t", n4)
        n2_t = load_list("n2_t", n2)
        n6_t = load_list("n6_t", n6)
        n5_t = load_list("n5_t", n5)

        xo_s = gather("xo_s", U8, xs[:], offs_t)
        xt_s = gather("xt_s", U8, xs[:], two_t)
        xo_w = gather("xo_w", U32, xw[:].bitcast(U32), offs_t)
        dk_s = gather("dk_s", U8, ds[:], kidx_t)
        w1_b = keep.tile([P, 2048], BF16, name="w1_b", align_bytes=64)
        w1_dealt = w1_b[:].rearrange("p (t m j) -> p m j t", t=PACK, j=PACK)
        for half in range(2):
            nc.scalar.copy(
                out=w1_dealt[:, 64 * half : 64 * (half + 1)],
                in_=w1_raw[half][:].rearrange("p j (m t) -> p m j t", t=PACK),
            )
        w1_q = quantize("w1", w1_b)
        dd_s = keep.tile([P, S], U8, name="dd_s", tag="dd_s", align_bytes=64)
        nc.vector.tensor_copy(
            out=dd_s[:].rearrange("p (t m) -> p t m", t=PACK), in_=dk_s[:].rearrange("p (m t) -> p t m", t=PACK)
        )
        for e in range(2):
            nc.sync.dma_start(out=dd_s[2 + e : P : 32, :].bitcast(I32), in_=dd_s[16 + e : P : 32, :].bitcast(I32))
        w3_raw = load_weight("w3_raw", "dk_s", w3)
        dk_w = gather("dk_w", U32, dw[:].bitcast(U32), kidx_t)
        xt_w = gather("xt_w", U32, xw[:].bitcast(U32), two_t, "w1_raw1")
        dd_w = keep.tile([P, S], U32, name="dd_w", tag="dd_w", align_bytes=64)
        nc.vector.tensor_copy(
            out=dd_w[:].rearrange("p (t m) -> p t m", t=PACK), in_=dk_w[:].rearrange("p (m t) -> p t m", t=PACK)
        )
        w2_b = keep.tile([P, 2048], BF16, name="w2_b", align_bytes=64)
        interleave(nc.vector.tensor_copy, w2_b, w2_raw)

        y_ps = [psum.tile([P, S], F32, name="y_ps%d" % t, tag="bank%d" % t) for t in range(PACK)]
        for t in range(PACK):
            product(y_ps[t], w1_q, slice(P * t, P * (t + 1)), (xo_w, xo_s), True, True)

        def tiles(name, width, dtype=F32):
            return [keep.tile([P, width], dtype, name="%s%d" % (name, t), tag="%s%d" % (name, t), align_bytes=64) for t in range(PACK)]

        th, ex, g3 = tiles("th", WIDE), tiles("ex", WIDE), tiles("gth", S)
        st = [None] * PACK
        num = keep.tile([P, PACK, S], F32, name="num")

        def held(name, tags):
            return [keep.tile([P, S], F32, name="%s%d" % (name, t), tag=tag, align_bytes=64) for t, tag in enumerate(tags)]

        def gate(t):
            nc.scalar.activation(sg[t][:], th[t][:].indirect(n1_t[:]), ACT.Copy, bias=0.5, scale=0.5)

        def gated(t):
            st[t] = keep.tile([P, WIDE], F32, name="st%d" % t, tag=("w2_raw", "ex1", "gth2", "ex2")[t], align_bytes=64)
            nc.vector.tensor_tensor(st[t][:, :S], sg[t][:], y_ps[t][:], ALU.mult)

        sg = held("sg", ("sg0",))
        for t in range(PACK):
            nc.scalar.activation(th[t][:, :S], y_ps[t][:], ACT.Tanh, scale=0.5)
        gate(0)
        gated(0)
        w2_q = quantize("w2", w2_b)
        w3_b = keep.tile([P, 2048], BF16, name="w3_b", align_bytes=64)
        interleave(nc.vector.tensor_copy, w3_b, w3_raw)
        rows = keep.tile([P, PACK + 2, S], F32, name="rows", tag="dk_s", align_bytes=64)
        den = rows[:, :PACK, :]
        ex2 = [rows[:, slot, :] for slot in (4, 2, 3, 5)]
        s_ps = [psum.tile([P, S], F32, name="s_ps%d" % t, tag="bank%d" % (PACK + t)) for t in range(PACK)]
        for t in range(PACK + 1):
            if t < PACK:
                product(s_ps[t], (dd_w, dd_s), slice(P * t, P * (t + 1)), (xt_w, xt_s), True, True)
                nc.scalar.activation(ex[t][:, :S], s_ps[t][:], ACT.Exp, scale=0.03125)
                nc.sync.dma_start(out=ex2[t], in_=ex[t][:, :S])
            if t > 0:
                nc.scalar.activation(g3[t - 1][:], ex[t - 1][:].indirect(n3_t[:]), ACT.Copy)
        sg.extend(held("late_sg", ("w1_raw1", "dd_w", "xt_s")))
        for t in range(1, PACK):
            gate(t)

        def denominator(t):
            nc.vector.tensor_tensor(den[:, t, :], ex[t][:].indirect(n4_t[:]), g3[t][:], ALU.add)

        def numerator(t):
            nc.vector.tensor_tensor(num[:, t, :], ex[t][:].indirect(n2_t[:]), ex2[t], ALU.add)

        denominator(0)
        w3_q = quantize("w3", w3_b)
        denominator(1)
        numerator(0)
        numerator(1)
        denominator(2)
        gated(1)
        gated(2)
        numerator(2)
        gated(3)
        denominator(3)
        numerator(3)
        stg = held("stg", ("dd_s", "stg1", "stg2", "stg3"))
        for t in range(PACK):
            nc.scalar.activation(stg[t][:], st[t][:].indirect(n1_t[:]), ACT.Copy)
        halves = [slice(HALF * half, HALF * (half + 1)) for half in range(2)]
        for cols in halves:
            nc.scalar.activation(den[:, :, cols], den[:, :, cols], ACT.Ln)
            nc.scalar.activation(num[:, :, cols], num[:, :, cols], ACT.Ln)
        warm = keep.tile([P, 8], F32, name="warm")
        nc.scalar.activation(warm[:, 0:1], den[:, PACK - 1, S - 1 : S], ACT.Abs_reciprocal_sqrt, bias=0.5)
        z_planes = keep.tile([P, PACK, S], F32, name="z_planes", tag="ex3", align_bytes=64)
        for t in range(PACK):
            nc.vector.tensor_tensor(z_planes[:, t, :], stg[t][:], st[t][:, :S], ALU.max)
        z_b = keep.tile([P, 2048], BF16, name="z_b", align_bytes=64)
        gain_and_group(z_b, z_planes, gn_t, 0, S)
        z2_codes = keep.tile([P, S], U32, name="z2_codes", align_bytes=64)
        z2_scales = keep.tile([P, S], U8, name="z2_scales", align_bytes=64)

        def quantize_z2(cols, grouped):
            nc.vector.quantize_mx(
                out=z2_codes[:, cols].bitcast(FP8X4),
                scales=z2_scales[:, cols],
                in_=grouped[:],
            )

        z2_lo = keep.tile([P, PACK * HALF], BF16, name="z2_lo", align_bytes=64)
        z2_hi = keep.tile([P, PACK * HALF], BF16, name="z2_hi", align_bytes=64)
        nc.vector.tensor_tensor(num[:, :, halves[0]], num[:, :, halves[0]], den[:, :, halves[0]], ALU.subtract)
        z_q = quantize("z", z_b)
        gain_and_group(z2_lo, num, gk_t, 0, HALF)
        nc.vector.tensor_tensor(num[:, :, halves[1]], num[:, :, halves[1]], den[:, :, halves[1]], ALU.subtract)
        quantize_z2(halves[0], z2_lo)
        gain_and_group(z2_hi, num, gk_t, HALF, S)
        quantize_z2(halves[1], z2_hi)

        h_ps = [psum.tile([P, S], F32, name="h_ps%d" % m, tag="bank%d" % (PACK + m)) for m in range(PACK)]
        for m in range(PACK):
            product(h_ps[m], w2_q, slice(P * m, P * (m + 1)), z_q, True, False)
        for half in range(2):
            for m in range(PACK):
                cols = slice(HALF * half, HALF * (half + 1))
                product(h_ps[m], w3_q, slice(P * m, P * (m + 1)), (z2_codes, z2_scales), False, half == 1, cols)

        h2, d6, root = tiles("hb", S), tiles("dsix", S), tiles("root", S)
        h = [keep.tile([P, WIDE * (2 if m == PACK - 1 else 1)], F32, name="h%d" % m) for m in range(PACK)]
        spare = [h[3][:, S * (i + 1) : S * (i + 2)] for i in range(3)]
        fetched = tiles("fetched", S)
        d5 = [fetched[0][:], spare[0], fetched[2][:], fetched[3][:]]
        result = [spare[1]] + [h2[m][:] for m in range(1, PACK)]
        inverse_root = [root[0][:], root[1][:], spare[2], root[3][:]]
        nc.vector.tensor_copy(h2[1][:], h_ps[1][:])
        for m in (0, 2, 3, 1):
            nc.scalar.copy(h[m][:, :S], h_ps[m][:])
            if m > 1:
                nc.sync.dma_start(out=h2[m][:], in_=h[m][:, :S])
        nc.vector.tensor_copy(h2[0][:], h[0][:, :S])

        def minus_h(dst, m, places):
            nc.vector.tensor_tensor(dst, h[m][:].indirect(places[:]), h2[m][:], ALU.subtract)

        for m in (2, 3):
            nc.scalar.activation(d5[m], h[m][:].indirect(n5_t[:]), ACT.Copy)
        for m in range(PACK):
            minus_h(d6[m][:], m, n6_t)
            if m == 1:
                minus_h(d5[0], 0, n5_t)
        for pair in ((0, 1), (2, 3)):
            for m in pair:
                nc.scalar.activation(d6[m][:], d6[m][:], ACT.Abs)
            for m in pair:
                nc.scalar.activation(inverse_root[m], d6[m][:], ACT.Abs_reciprocal_sqrt, bias=0.5)
            for m in pair:
                nc.scalar.activation(d6[m][:], inverse_root[m], ACT.Square)
        minus_h(d5[1], 1, n5_t)
        for m in (2, 3):
            nc.vector.tensor_tensor(d5[m], d5[m], h2[m][:], ALU.subtract)
        for m in range(PACK):
            nc.vector.scalar_tensor_tensor(result[m], d5[m], -1.0, d6[m][:], ALU.mult, ALU.mult)
            nc.sync.dma_start(out=out[P * m : P * (m + 1), :], in_=result[m])
